import numpy as np
import ml_dtypes


def mxq(x, axis, fmt="e4m3"):
    dtype, down = {"e4m3": (ml_dtypes.float8_e4m3fn, 7), "e5m2": (ml_dtypes.float8_e5m2, 14)}[fmt]
    v = np.moveaxis(np.asarray(x, np.float32).astype(ml_dtypes.bfloat16).astype(np.float64), axis, -1)
    blocks = v.reshape(v.shape[:-1] + (-1, 32))
    amax = np.abs(blocks).max(-1, keepdims=True)
    byte = np.maximum(np.where(amax > 0, np.frexp(amax)[1] - 1 + 127, 0) - down, 1)
    scale = np.exp2(byte - 127.0)
    codes = (blocks / scale).astype(np.float32).astype(dtype).astype(np.float64)
    return np.moveaxis((codes * scale).reshape(v.shape), -1, axis)


WIDE = False


def mx_kscale(k):
    if not WIDE:
        return np.ones(k)
    levels = np.array([30, -30])
    if k % 512:
        return np.exp2(np.random.permutation(np.resize(levels, k // 32))).repeat(32)
    a = np.empty((k // 512, 16))
    for p in range(k // 512):
        a[p, :8] = np.random.permutation(np.resize(levels, 8))
        for g in range(8):
            far = levels[np.abs(levels - a[p, g]) >= 10]
            a[p, g + 8] = far[np.random.randint(len(far))]
    return np.exp2(a.ravel()).repeat(32)


BF16 = ml_dtypes.bfloat16


def bf(x):
    return np.asarray(x, np.float32).astype(BF16)


def f64(x):
    return np.asarray(x).astype(np.float64)


M, K, F, N = 1024, 1536, 512, 2048


def sigmoid(z):
    return 1.0 / (1.0 + np.exp(-z))


def setup_inputs():
    s, t = mx_kscale(K), mx_kscale(F)
    return {"x": bf(np.random.standard_normal((M, K)) * s),
            "wv": bf(np.random.standard_normal((K, F)) / np.sqrt(K) / s[:, None]),
            "bv": bf(0.3 * np.random.standard_normal(F)),
            "wg": bf(np.random.standard_normal((K, F)) / np.sqrt(K) / s[:, None]),
            "bg": bf(0.5 * np.random.standard_normal(F)),
            "gain": bf((1.0 + 0.1 * np.random.standard_normal(F)) * t),
            "docs": bf(np.random.standard_normal((N, F)) / np.sqrt(F) / t),
            "log_tau": bf(0.2 * np.random.standard_normal(M)),
            "prior": bf(0.4 * np.random.standard_normal(N))}


def reference(x, wv, bv, wg, bg, gain, docs, log_tau, prior):
    xq = mxq(f64(x), 1, "e4m3")
    v = (xq @ mxq(f64(wv), 0, "e4m3")) + f64(bv)
    z = (xq @ mxq(f64(wg), 0, "e4m3")) + f64(bg)
    h = v * sigmoid(z)
    e = h / np.sqrt(np.mean(h * h, axis=1, keepdims=True)) * f64(gain)
    score = mxq(e, 1, "e5m2") @ mxq(f64(docs), 1, "e4m3").T
    logit = score * np.exp(-f64(log_tau))[:, None] + f64(prior)
    p = np.exp(logit - np.max(logit, axis=1, keepdims=True))
    return N * p / np.sum(p, axis=1, keepdims=True)

@@ -1,0 +1,411 @@
+from contextlib import ExitStack
+
+import concourse.mybir as mybir
+from concourse.masks import make_identity
+
+M, K, F, N = 1024, 1536, 512, 2048
+FLOPS = 2 * M * K * 2 * F + 2 * M * F * N
+P = 128
+PACK = 4
+KG = K // 512
+TILES = M // P
+CHUNK = 512
+CHUNKS = N // CHUNK
+GROUP_SIZES = (1, 1, 2, 2, 2)
+NARROW = (2, 2, 2, 2, 2, 2, 2, 2)
+LIFT = (((0, 2048, "G"),), ((0, 2048, "G"),), ((0, 2048, "G"),), ((0, 2048, "G"),), ((0, 2048, "G"),), ((0, 2048, "G"),), ((0, 2048, "G"),), ((0, 1024, "V"), (1024, 1536, "S"), (1536, 2048, "G")))
+WENG = "VVVSVS"
+XENG = "SSSSS"
+DENG = "SSSSSSSS"
+EENG = "VVVVV"
+HENG = "GGSSS"
+NENG = "S"
+PREADD = 1
+ORDER = {
+    "V": "dq0 pc0 Iz0 Iz1 Iz2 Qz1 xq0a xq0b Qz0 Qz2 xq1a xq1b Iv1 pc2 Qv0 Qv1 Qv2 xq2a dq1 dq2 xq2b xq2c h0a h1a xq3a h2a e0 qe0 xq3b dq3 xq3c xq4a l0_0 l0_1 l0_2 l0_3 h2b e1 xq4b qe1 lw0 l1_0 l1_1 h3a l1_2 xq4c h3b l1_3 lw1 ln0 ln1 e2 qe2 h4a l2_0 h4b l2_1 l2_2 inv0 l2_3 lw2 l3_0 l3_1 l3_2 inv1 ln2 e3 l3_3 qe3 lw3 inv2 ln3 l4_0 l4_1 l4_2 l4_3 lw4 e4 ln4 inv3 qe4 l5_0 l5_1 l5_2 l5_3 inv4 lw5 ln5 l6_0 l6_1 l6_2 l6_3 lw6 l7_0 ln6 inv5 l7_1 l7_2 l7_3 lw7 inv6 ln7 inv7 f7_0",
+    "S": "cd0a pc1 cd0b cd1a cd1b cd2a pc3 cd2b cx0a cx0b cx1a cx1b Iv0 Iv2 cx2a cx2b cx2c sig0a cd3a sig1a sq0a sq1a cx3a sig2a mean0 cd3b hg2a cx3b cx3c cx4a mean1 sig2b n0_0 n0_1 cx4b sq2a hg2b sq2b cx4c sig3a n1_0 sig3b sq3a hg3a n1_1 mean2 sq3b sig4a sig4b exp0 mean3 exp1 n2_0 sq4a sq4b n2_1 hg3b n3_0 exp2 n3_1 hg4a mean4 exp3 hg4b n4_0 n4_1 exp4 n5_0 n5_1 exp5 n6_0 n6_1 n7_0 exp6 n7_1 exp7 f7_1",
+    "T": "td0a pm0 pm1 td0b td1a pm2 td1b td2a pm3 td2b tx0a tx0b tx1a tx1b td3a td3b z0a z1a tx2a tx2b tx2c tx3a v0a v1a z2a v2a z2b ms0 tx3b tx3c spread0 tx4a tx4b ms1 s0_0 s0_1 s0_2 v2b s0_3 v3a spread1 tx4c z3a s1_0 s1_1 z3b s1_2 s1_3 v3b ms2 z4a z4b spread2 v4a v4b s2_0 ms3 s2_1 s2_2 s2_3 s3_0 s3_1 s3_2 s3_3 spread3 s4_0 s4_1 s4_2 ms4 s4_3 s5_0 s5_1 s5_2 spread4 s5_3 s6_0 s6_1 s6_2 s6_3 s7_0 s7_1 s7_2 s7_3",
+    "G": "hg0a add0 pow0 add1 pow1 hg1a add2 pow2 add3 pow3 f0_0 add4 f1_0 pow4 f2_0 f3_0 f4_0 f5_0 f6_0 f7_2",
+}
+
+F32 = mybir.dt.float32
+BF16 = mybir.dt.bfloat16
+U32 = mybir.dt.uint32
+U8 = mybir.dt.uint8
+E4M3X4 = mybir.dt.float8_e4m3fn_x4
+E5M2X4 = mybir.dt.float8_e5m2_x4
+ALU = mybir.AluOpType
+ACT = mybir.ActivationFunctionType
+
+
+def tile_gated_query_retrieval_f3_kernel(tc, x, wv, bv, wg, bg, gain, docs, log_tau, prior, out):
+    nc = tc.nc
+    x_rows = x.rearrange("(p t) k -> t p k", t=TILES)
+    out_rows = out.rearrange("(p t) n -> t p n", t=TILES)
+    w_rows = {"z": wg.rearrange("(g p j) f -> g p j f", p=P, j=PACK), "v": wv.rearrange("(g p j) f -> g p j f", p=P, j=PACK)}
+    doc_rows = docs.rearrange("(c r p) f -> c p r f", c=CHUNKS, p=P)
+    groups = []
+    for n in GROUP_SIZES:
+        groups.append((sum(GROUP_SIZES[:len(groups)]), n))
+    where = {}
+    for g, (first, n) in enumerate(groups):
+        for b in range(n):
+            where[first + b] = (g, b)
+
+    with ExitStack() as ctx:
+        keep = ctx.enter_context(tc.tile_pool(name="keep", bufs=1))
+        work = ctx.enter_context(tc.tile_pool(name="work", bufs=2))
+        raw = ctx.enter_context(tc.tile_pool(name="raw", bufs=8))
+        soft = ctx.enter_context(tc.tile_pool(name="soft", bufs=2))
+        lots = ctx.enter_context(tc.tile_pool(name="lots", bufs=4))
+        banks = ctx.enter_context(tc.psum_pool(name="banks", bufs=7))
+        rms = ctx.enter_context(tc.psum_pool(name="rms", bufs=1))
+
+        prior_row = raw.tile([P, N], BF16, name="prior_row", tag="raw", align_bytes=64)
+        nc.vector.memset(prior_row[:], 0.0)
+        ones = keep.tile([P, P], BF16, name="ones")
+        nc.vector.memset(ones[:], 1.0)
+        ident = keep.tile([P, P], F32, name="ident")
+        make_identity(nc, ident[:])
+        inv_f = keep.tile([P, 2], F32, name="inv_f")
+        nc.gpsimd.memset(inv_f[:], 1.0 / F)
+        minus_half = keep.tile([P, 2], F32, name="minus_half")
+        nc.gpsimd.memset(minus_half[:], -0.5)
+
+        bv_sb = keep.tile([P, PACK], BF16, name="bv_sb")
+        bg_sb = keep.tile([P, PACK], BF16, name="bg_sb")
+        gain_sb = keep.tile([P, PACK], BF16, name="gain_sb")
+        gain32 = keep.tile([P, PACK], F32, name="gain32")
+        lt_sb = keep.tile([P, TILES], BF16, name="lt_sb")
+        inv_tau = keep.tile([P, TILES], F32, name="inv_tau")
+        neg_inv_tau = keep.tile([P, TILES], F32, name="neg_inv_tau")
+        prior_sb = keep.tile([P, N], BF16, name="prior_sb")
+        warm = keep.tile([P, 1], F32, name="warm")
+        mean_sq = keep.tile([P, TILES], F32, name="mean_sq")
+        rstd = keep.tile([P, TILES], F32, name="rstd")
+        low = keep.tile([P, TILES], F32, name="low")
+        part_low = keep.tile([P, TILES], F32, name="part_low")
+        total = keep.tile([P, TILES], F32, name="total")
+        share = keep.tile([P, TILES], F32, name="share")
+        scaled = keep.tile([P, TILES], F32, name="scaled")
+
+        w_raw, d_raw, w_grp, w_codes, w_scales = {}, {}, {}, {}, {}
+        for which in ("z", "v"):
+            for g in range(KG):
+                tagname = "%s%d" % (which, g)
+                w_codes[which, g] = keep.tile([P, F], U32, name="w_codes_" + tagname, align_bytes=64)
+                w_scales[which, g] = keep.tile([P, F], U8, name="w_scales_" + tagname, align_bytes=64)
+        x_raw = {}
+        x_codes = [keep.tile([P, KG, n * P], U32, name="x_codes%d" % g, align_bytes=64) for g, (first, n) in enumerate(groups)]
+        x_scales = [keep.tile([P, KG, n * P], U8, name="x_scales%d" % g, align_bytes=64) for g, (first, n) in enumerate(groups)]
+        d_codes = [keep.tile([P, CHUNK], U32, name="d_codes%d" % c, align_bytes=64) for c in range(CHUNKS)]
+        d_scales = [keep.tile([P, CHUNK], U8, name="d_scales%d" % c, align_bytes=64) for c in range(CHUNKS)]
+        e_codes = [keep.tile([P, n * P], U32, name="e_codes%d" % g, align_bytes=64) for g, (first, n) in enumerate(groups)]
+        e_scales = [keep.tile([P, n * P], U8, name="e_scales%d" % g, align_bytes=64) for g, (first, n) in enumerate(groups)]
+        bank_of, grp_of, sig, h, hg, sq, sums, bc, bcs, e_bf, d_grp, neg, nb, pb = {}, {}, {}, {}, {}, {}, {}, {}, {}, {}, {}, {}, {}, {}
+        copy_on = {"V": nc.vector.tensor_copy, "S": nc.scalar.copy}
+
+        def load_w(which, g):
+            w_raw[which, g] = raw.tile([P, PACK, F], BF16, name="raw", align_bytes=64)
+            nc.sync.dma_start(out=w_raw[which, g][:], in_=w_rows[which][g])
+
+        def load_x(i):
+            x_raw[i] = raw.tile([P, K], BF16, name="x_raw", bufs=6, align_bytes=64)
+            nc.sync.dma_start(out=x_raw[i][:], in_=x_rows[i])
+
+        def load_d(c):
+            d_raw[c] = raw.tile([P, 4, F], BF16, name="raw", align_bytes=64)
+            nc.sync.dma_start(out=d_raw[c][:], in_=doc_rows[c])
+
+        def spread_prior(c):
+            pb[c] = banks.tile([P, CHUNK], F32, name="bank_p", tag="bank")
+            nc.tensor.matmul(out=pb[c][:], lhsT=ones[:], rhs=prior_row[:, c * CHUNK:(c + 1) * CHUNK], start=True, stop=True)
+
+        def copy_prior(c):
+            copy_on["VS"[c % 2]](out=prior_sb[:, c * CHUNK:(c + 1) * CHUNK], in_=pb[c][:])
+
+        def interleave(which, g, engine):
+            w_grp[which, g] = soft.tile([P, F * PACK], BF16, name="w_grp", tag="w_grp" + engine, bufs=3 if engine == "V" else 2, align_bytes=64)
+            copy_on[engine](out=w_grp[which, g][:].rearrange("p (t m j) -> p t m j", t=PACK, j=PACK),
+                 in_=w_raw[which, g][:].rearrange("p j (m t) -> p t m j", t=PACK))
+
+        def quant_w(which, g):
+            nc.vector.quantize_mx(out=w_codes[which, g][:].bitcast(E4M3X4), scales=w_scales[which, g][:], in_=w_grp[which, g][:])
+
+        def slots_of(g, k):
+            n = groups[g][1]
+            if n == 2:
+                return [(k, 0), (k, 1)]
+            return [(0, 0), (1, 0)] if k == 0 else [(2, 0)]
+
+        def turn_x(g, k):
+            slots = slots_of(g, k)
+            bank = banks.tile([P, len(slots), 2, P], F32, name="bank_x", tag="bank")
+            for s, (kg, b) in enumerate(slots):
+                words = x_raw[groups[g][0] + b][:].bitcast(F32)
+                for u in range(2):
+                    nc.tensor.transpose(bank[:, s, u, :], words[:, 256 * kg + u:256 * (kg + 1):2], ident[:])
+            bank_of["x", g, k] = bank
+
+        def copy_x(g, k):
+            n = len(slots_of(g, k))
+            grp_of[g, k] = work.tile([P, n * P * PACK], BF16, name="x_grp", bufs=4, align_bytes=64)
+            copy_on[XENG[g]](out=grp_of[g, k][:].bitcast(F32).rearrange("p (c r u) -> p c r u", c=n, u=2), in_=bank_of["x", g, k][:].rearrange("p c u r -> p c r u"))
+
+        def quant_x(g, k):
+            if groups[g][1] == 2:
+                codes, scales = x_codes[g][:, k, :], x_scales[g][:, k, :]
+            else:
+                kg = slice(0, 2) if k == 0 else slice(2, 3)
+                codes, scales = x_codes[g][:, kg, :].rearrange("p g m -> p (g m)"), x_scales[g][:, kg, :].rearrange("p g m -> p (g m)")
+            nc.vector.quantize_mx(out=codes.bitcast(E4M3X4), scales=scales, in_=grp_of[g, k][:])
+
+        def project(which, g, part):
+            n = groups[g][1]
+            m = PACK // n
+            bank = banks.tile([P, m, n * P], F32, name="bank_" + which, tag="bank")
+            for s in range(m):
+                t = part * m + s
+                cols = slice(t * P, (t + 1) * P)
+                for k in range(KG):
+                    nc.tensor.matmul_mx(
+                        out=bank[:, s, :],
+                        lhsT=w_codes[which, k][:, cols].bitcast(E4M3X4), lhsT_scale=w_scales[which, k][:, cols],
+                        rhs=x_codes[g][:, k, :].bitcast(E4M3X4), rhs_scale=x_scales[g][:, k, :],
+                        start=(k == 0), stop=(k == KG - 1))
+            bank_of[which, g, part] = bank
+
+        def rows_of(store, g, name, bufs):
+            if g not in store:
+                store[g] = work.tile([P, PACK, groups[g][1] * P], F32, name=name, tag="%s%d" % (name, groups[g][1]), bufs=bufs[groups[g][1] - 1])
+            return store[g]
+
+        def each_t(g, part):
+            m = PACK // groups[g][1]
+            return [(part * m + s, s) for s in range(m)]
+
+        def sigmoid(g, part):
+            to = rows_of(sig, g, "sig", (2, 3))
+            for t, s in each_t(g, part):
+                nc.scalar.activation(out=to[:, t, :], in_=bank_of["z", g, part][:, s, :], func=ACT.Sigmoid, bias=bg_sb[:, t:t + 1])
+
+        def gate(g, part):
+            to = rows_of(h, g, "h", (2, 2))
+            for t, s in each_t(g, part):
+                nc.vector.scalar_tensor_tensor(out=to[:, t, :], in0=bank_of["v", g, part][:, s, :], scalar=bv_sb[:, t:t + 1], in1=sig[g][:, t, :], op0=ALU.add, op1=ALU.mult)
+
+        def gained(g, part):
+            to = rows_of(hg, g, "hg", (2, 2))
+            for t, s in each_t(g, part):
+                if HENG[g] == "G":
+                    nc.gpsimd.tensor_scalar(out=to[:, t, :], in0=h[g][:, t, :], scalar1=gain_sb[:, t:t + 1], scalar2=0.0, op0=ALU.mult, op1=ALU.add)
+                else:
+                    nc.scalar.activation(out=to[:, t, :], in_=h[g][:, t, :], func=ACT.Copy, scale=gain32[:, t:t + 1])
+
+        def square(g, part):
+            to = rows_of(sq, g, "sq", (2, 2))
+            m = PACK // groups[g][1]
+            nc.scalar.activation(out=to[:, part * m:(part + 1) * m, :], in_=h[g][:, part * m:(part + 1) * m, :], func=ACT.Square)
+
+        def add_up(g):
+            n = groups[g][1]
+            half = work.tile([P, 2, n * P], F32, name="half", tag="half%d" % n, bufs=1)
+            nc.gpsimd.tensor_tensor(out=half[:], in0=sq[g][:, 0:2, :], in1=sq[g][:, 2:4, :], op=ALU.add)
+            sums[g] = work.tile([P, n * P], F32, name="sums", tag="sums%d" % n)
+            nc.gpsimd.tensor_tensor(out=sums[g][:], in0=half[:, 0, :], in1=half[:, 1, :], op=ALU.add)
+
+        def mean_square(g):
+            n = groups[g][1]
+            bc[g] = rms.tile([P, 2 * P + 2], F32, name="bc")
+            for b in range(n):
+                parts = [sums[g][:, b * P:(b + 1) * P]] if PREADD else [sq[g][:, t, b * P:(b + 1) * P] for t in range(PACK)]
+                for t in range(len(parts)):
+                    nc.tensor.matmul(out=bc[g][:, 2 * P + b:2 * P + b + 1], lhsT=parts[t], rhs=inv_f[:, 0:1], start=(t == 0), stop=(t == len(parts) - 1))
+
+        def mean_copy(g):
+            first, n = groups[g]
+            nc.scalar.copy(out=mean_sq[:, first:first + n], in_=bc[g][:, 2 * P:2 * P + n])
+
+        def raise_power(g):
+            first, n = groups[g]
+            nc.gpsimd.tensor_tensor(out=rstd[:, first:first + n], in0=mean_sq[:, first:first + n], in1=minus_half[:, 0:n], op=ALU.pow)
+
+        def spread(g):
+            first, n = groups[g]
+            for b in range(n):
+                nc.tensor.matmul(out=bc[g][:, b * P:(b + 1) * P], lhsT=rstd[:, first + b:first + b + 1].to_broadcast([P, P]), rhs=ident[:], start=True, stop=True)
+
+        def carry(g):
+            w = groups[g][1] * P
+            bcs[g] = work.tile([P, w], F32, name="bcs", tag="bcs%d" % groups[g][1])
+            nc.scalar.copy(out=bcs[g][:], in_=bc[g][:, 0:w])
+
+        def embed(g):
+            w = groups[g][1] * P
+            e_bf[g] = work.tile([P, w, PACK], BF16, name="e_bf", tag="e_bf%d" % groups[g][1], align_bytes=64)
+            engine, factor = (nc.vector, bc[g]) if EENG[g] == "V" else (nc.gpsimd, bcs[g])
+            engine.tensor_tensor(out=e_bf[g][:], in0=hg[g][:].rearrange("p t n -> p n t"), in1=factor[:, 0:w].unsqueeze(2).to_broadcast([P, w, PACK]), op=ALU.mult)
+
+        def quant_e(g):
+            nc.vector.quantize_mx(out=e_codes[g][:].bitcast(E5M2X4), scales=e_scales[g][:], in_=e_bf[g][:].rearrange("p n t -> p (n t)"))
+
+        def turn_d(c, half):
+            bank = banks.tile([P, 2, 2, P], F32, name="bank_d", tag="bank")
+            for b in range(2):
+                words = d_raw[c][:, 2 * half + b, :].bitcast(F32)
+                for u in range(2):
+                    nc.tensor.transpose(bank[:, b, u, :], words[:, u:256:2], ident[:])
+            bank_of["d", c, half] = bank
+
+        def copy_d(c, half):
+            if c not in d_grp:
+                d_grp[c] = work.tile([P, CHUNK * PACK], BF16, name="d_grp", align_bytes=64)
+            copy_on[DENG[2 * c + half]](out=d_grp[c][:, half * 1024:(half + 1) * 1024].bitcast(F32).rearrange("p (b r u) -> p b r u", b=2, u=2), in_=bank_of["d", c, half][:].rearrange("p b u r -> p b r u"))
+
+        def quant_d(c):
+            nc.vector.quantize_mx(out=d_codes[c][:].bitcast(E4M3X4), scales=d_scales[c][:], in_=d_grp[c][:])
+
+        def score(i, c):
+            g, b = where[i]
+            cols = slice(b * P, (b + 1) * P)
+            bank_of["s", i, c] = banks.tile([P, CHUNK], F32, name="bank_s", tag="bank")
+            nc.tensor.matmul_mx(out=bank_of["s", i, c][:], lhsT=e_codes[g][:, cols].bitcast(E5M2X4), lhsT_scale=e_scales[g][:, cols],
+                                rhs=d_codes[c][:].bitcast(E4M3X4), rhs_scale=d_scales[c][:], start=True, stop=True)
+
+        def logit(i, c):
+            if i not in neg:
+                neg[i] = lots.tile([P, N], F32, name="neg")
+            cols = slice(c * CHUNK, (c + 1) * CHUNK)
+            nc.vector.scalar_tensor_tensor(out=neg[i][:, cols], in0=bank_of["s", i, c][:], scalar=neg_inv_tau[:, i:i + 1], in1=prior_sb[:, cols], op0=ALU.mult, op1=ALU.subtract)
+
+        def narrow(i, c):
+            if i not in nb:
+                nb[i] = soft.tile([P, NARROW[i] * CHUNK], BF16, name="nb", tag="nb%d" % NARROW[i])
+            cols = slice(c * CHUNK, (c + 1) * CHUNK)
+            if NENG == "S":
+                nc.scalar.copy(out=nb[i][:, cols], in_=neg[i][:, cols])
+            else:
+                nc.gpsimd.tensor_scalar(out=nb[i][:, cols], in0=neg[i][:, cols], scalar1=1.0, scalar2=0.0, op0=ALU.mult, op1=ALU.add)
+
+        def low_wide(i):
+            to = part_low if NARROW[i] else low
+            nc.vector.tensor_reduce(out=to[:, i:i + 1], in_=neg[i][:, NARROW[i] * CHUNK:N], axis=mybir.AxisListType.X, op=ALU.min)
+
+        def low_narrow(i):
+            start = part_low[:, i:i + 1] if NARROW[i] < CHUNKS else None
+            nc.vector.tensor_scalar(out=nb[i][:], in0=nb[i][:], scalar1=1.0, scalar2=start, op0=ALU.mult, op1=ALU.min, accum_out=low[:, i:i + 1])
+
+        def exponent(i):
+            nc.scalar.activation(out=neg[i][:], in_=neg[i][:], func=ACT.Exp, scale=-1.0, bias=low[:, i:i + 1], accum_out=total[:, i:i + 1])
+
+        def invert(i):
+            nc.vector.reciprocal(out=share[:, i:i + 1], in_=total[:, i:i + 1])
+            if any(cut[2] == "S" for cut in LIFT[i]):
+                nc.vector.tensor_scalar(out=scaled[:, i:i + 1], in0=share[:, i:i + 1], scalar1=float(N), scalar2=0.0, op0=ALU.mult, op1=ALU.add)
+
+        def lift(i, k):
+            lo, hi, engine = LIFT[i][k]
+            a = neg[i][:, lo:hi]
+            if engine == "S":
+                nc.scalar.activation(out=a, in_=a, func=ACT.Copy, scale=scaled[:, i:i + 1])
+            else:
+                (nc.vector if engine == "V" else nc.gpsimd).tensor_scalar(out=a, in0=a, scalar1=share[:, i:i + 1], scalar2=float(N), op0=ALU.mult, op1=ALU.mult)
+            nc.sync.dma_start(out=out_rows[i][:, lo:hi], in_=a)
+
+        needs, emit = {}, {}
+
+        def piece(name, deps, f, *args):
+            emit[name] = (f, args)
+            needs[name] = deps
+
+        for c in range(CHUNKS):
+            piece("pm%d" % c, [], spread_prior, c)
+            piece("pc%d" % c, ["pm%d" % c], copy_prior, c)
+        for k in range(6):
+            which, g = "zv"[k // 3], k % 3
+            w = "%s%d" % (which, g)
+            piece("I" + w, [], interleave, which, g, WENG[k])
+            piece("Q" + w, ["I" + w], quant_w, which, g)
+        for g, (first, n) in enumerate(groups):
+            name = str(g)
+            turns = range(3) if n == 2 else range(2)
+            for k in turns:
+                piece("tx" + name + "abc"[k], [], turn_x, g, k)
+                piece("cx" + name + "abc"[k], ["tx" + name + "abc"[k]], copy_x, g, k)
+                piece("xq" + name + "abc"[k], ["cx" + name + "abc"[k]], quant_x, g, k)
+            ready = ["xq" + name + "abc"[k] for k in turns]
+            parts = ["ab"[b] for b in range(n)]
+            for b, a in enumerate(parts):
+                for which in "zv":
+                    piece(which + name + a, ready + ["Q%s%d" % (which, k) for k in range(KG)], project, which, g, b)
+                piece("sig" + name + a, ["z" + name + a], sigmoid, g, b)
+                piece("h" + name + a, ["v" + name + a, "sig" + name + a], gate, g, b)
+                piece("hg" + name + a, ["h" + name + a], gained, g, b)
+                piece("sq" + name + a, ["h" + name + a], square, g, b)
+            piece("add" + name, ["sq" + name + a for a in parts], add_up, g)
+            piece("ms" + name, ["add" + name] if PREADD else ["sq" + name + a for a in parts], mean_square, g)
+            piece("mean" + name, ["ms" + name], mean_copy, g)
+            piece("pow" + name, ["mean" + name], raise_power, g)
+            piece("spread" + name, ["pow" + name], spread, g)
+            piece("carry" + name, ["spread" + name], carry, g)
+            piece("e" + name, [("spread" if EENG[g] == "V" else "carry") + name] + ["hg" + name + a for a in parts], embed, g)
+            piece("qe" + name, ["e" + name], quant_e, g)
+            for i in range(first, first + n):
+                for c in range(CHUNKS):
+                    piece("s%d_%d" % (i, c), ["qe" + name, "dq%d" % c], score, i, c)
+                    piece("l%d_%d" % (i, c), ["s%d_%d" % (i, c), "pc%d" % c], logit, i, c)
+                    piece("n%d_%d" % (i, c), ["l%d_%d" % (i, c)], narrow, i, c)
+                piece("lw%d" % i, ["l%d_%d" % (i, c) for c in range(NARROW[i], CHUNKS)], low_wide, i)
+                piece("ln%d" % i, ["n%d_%d" % (i, c) for c in range(NARROW[i])] + (["lw%d" % i] if NARROW[i] < CHUNKS else []), low_narrow, i)
+                piece("exp%d" % i, [("ln%d" if NARROW[i] else "lw%d") % i], exponent, i)
+                piece("inv%d" % i, ["exp%d" % i], invert, i)
+                for k in range(len(LIFT[i])):
+                    piece("f%d_%d" % (i, k), ["inv%d" % i], lift, i, k)
+        for c in range(CHUNKS):
+            for half in range(2):
+                hn = "%d%s" % (c, "ab"[half])
+                piece("td" + hn, [], turn_d, c, half)
+                piece("cd" + hn, ["td" + hn], copy_d, c, half)
+            piece("dq%d" % c, ["cd%da" % c, "cd%db" % c], quant_d, c)
+
+        with tc.manual_schedule():
+            nc.scalar.dma_start(out=lt_sb[:], in_=log_tau.rearrange("(p t) -> p t", t=TILES))
+            nc.scalar.dma_start(out=bg_sb[:], in_=bg.rearrange("(p t) -> p t", t=PACK))
+            nc.scalar.dma_start(out=bv_sb[:], in_=bv.rearrange("(p t) -> p t", t=PACK))
+            nc.scalar.dma_start(out=gain_sb[:], in_=gain.rearrange("(p t) -> p t", t=PACK))
+            nc.scalar.dma_start(out=prior_row[0:1, :], in_=prior.unsqueeze(0))
+            load_d(0)
+            load_d(1)
+            load_d(2)
+            load_d(3)
+            load_w("z", 0)
+            load_w("z", 1)
+            load_w("z", 2)
+            load_x(0)
+            load_x(1)
+            load_w("v", 0)
+            load_w("v", 1)
+            load_w("v", 2)
+            load_x(2)
+            load_x(3)
+            load_x(4)
+            load_x(5)
+            load_x(6)
+            load_x(7)
+            nc.scalar.activation(out=inv_tau[:], in_=lt_sb[:], func=ACT.Exp, scale=-1.0)
+            nc.scalar.activation(out=warm[:], in_=inv_tau[:, 0:1], func=ACT.Sigmoid)
+            nc.gpsimd.tensor_scalar(out=neg_inv_tau[:], in0=inv_tau[:], scalar1=-1.0, scalar2=0.0, op0=ALU.mult, op1=ALU.add)
+            nc.gpsimd.tensor_copy(out=gain32[:], in_=gain_sb[:])
+            queues = {e: names.split() for e, names in ORDER.items()}
+            done = set()
+            left = sum(len(q) for q in queues.values())
+            while left:
+                before = left
+                for e in queues:
+                    while queues[e] and all(d in done for d in needs[queues[e][0]]):
+                        name = queues[e].pop(0)
+                        f, args = emit[name]
+                        f(*args)
+                        done.add(name)
+                        left -= 1
+                assert left < before

@@ -22,10 +22,10 @@ HENG = "GGSSS"
 NENG = "S"
 PREADD = 1
 ORDER = {
-    "V": "dq0 pc0 Iz0 Iz1 Iz2 Qz1 xq0a xq0b Qz0 Qz2 xq1a xq1b Iv1 pc2 Qv0 Qv1 Qv2 xq2a dq1 dq2 xq2b xq2c h0a h1a xq3a h2a e0 qe0 xq3b dq3 xq3c xq4a l0_0 l0_1 l0_2 l0_3 h2b e1 xq4b qe1 lw0 l1_0 l1_1 h3a l1_2 xq4c h3b l1_3 lw1 ln0 ln1 e2 qe2 h4a l2_0 h4b l2_1 l2_2 inv0 l2_3 lw2 l3_0 l3_1 l3_2 inv1 ln2 e3 l3_3 qe3 lw3 inv2 ln3 l4_0 l4_1 l4_2 l4_3 lw4 e4 ln4 inv3 qe4 l5_0 l5_1 l5_2 l5_3 inv4 lw5 ln5 l6_0 l6_1 l6_2 l6_3 lw6 l7_0 ln6 inv5 l7_1 l7_2 l7_3 lw7 inv6 ln7 inv7 f7_0",
-    "S": "cd0a pc1 cd0b cd1a cd1b cd2a pc3 cd2b cx0a cx0b cx1a cx1b Iv0 Iv2 cx2a cx2b cx2c sig0a cd3a sig1a sq0a sq1a cx3a sig2a mean0 cd3b hg2a cx3b cx3c cx4a mean1 sig2b n0_0 n0_1 cx4b sq2a hg2b sq2b cx4c sig3a n1_0 sig3b sq3a hg3a n1_1 mean2 sq3b sig4a sig4b exp0 mean3 exp1 n2_0 sq4a sq4b n2_1 hg3b n3_0 exp2 n3_1 hg4a mean4 exp3 hg4b n4_0 n4_1 exp4 n5_0 n5_1 exp5 n6_0 n6_1 n7_0 exp6 n7_1 exp7 f7_1",
-    "T": "td0a pm0 pm1 td0b td1a pm2 td1b td2a pm3 td2b tx0a tx0b tx1a tx1b td3a td3b z0a z1a tx2a tx2b tx2c tx3a v0a v1a z2a v2a z2b ms0 tx3b tx3c spread0 tx4a tx4b ms1 s0_0 s0_1 s0_2 v2b s0_3 v3a spread1 tx4c z3a s1_0 s1_1 z3b s1_2 s1_3 v3b ms2 z4a z4b spread2 v4a v4b s2_0 ms3 s2_1 s2_2 s2_3 s3_0 s3_1 s3_2 s3_3 spread3 s4_0 s4_1 s4_2 ms4 s4_3 s5_0 s5_1 s5_2 spread4 s5_3 s6_0 s6_1 s6_2 s6_3 s7_0 s7_1 s7_2 s7_3",
-    "G": "hg0a add0 pow0 add1 pow1 hg1a add2 pow2 add3 pow3 f0_0 add4 f1_0 pow4 f2_0 f3_0 f4_0 f5_0 f6_0 f7_2",
+    "V": "Iz0 Iz1 Qz0 Qz1 Iz2 xq0a xq0b Qz2 xq1a xq1b Iv1 pc0 Qv0 Qv1 pc2 Qv2 dq0 h0a dq1 h1a e0 xq2a qe0 xq2b xq2c xq3a dq2 l0_0 xq3b xq3c xq4a l0_1 dq3 l0_2 h2a h2b l0_3 e1 xq4b qe1 lw0 h3a l1_0 ln0 xq4c h3b l1_1 l1_2 l1_3 lw1 e2 h4a qe2 ln1 h4b l2_0 l2_1 inv0 l2_2 l2_3 l3_0 l3_1 l3_2 lw2 e3 inv1 qe3 l3_3 ln2 lw3 l4_0 ln3 l4_1 inv2 l4_2 l4_3 e4 inv3 lw4 l5_0 ln4 l5_1 l5_2 l5_3 qe4 lw5 inv4 l6_0 ln5 l6_1 l6_2 l6_3 l7_0 lw6 l7_1 ln6 l7_2 l7_3 inv5 lw7 ln7 inv6 inv7 f7_0",
+    "S": "pc1 cx0a cx0b cx1a cx1b Iv0 Iv2 cd0a cd0b cd1a sig0a cd1b sig1a sq0a sq1a cx2a cx2b cd2a mean0 cd2b cd3a pc3 cx2c cx3a cd3b cx3b cx3c cx4a mean1 n0_0 sig2a n0_1 cx4b sig2b sq2a hg2a sq2b sig3a hg2b cx4c sig3b sq3a hg3a mean2 n1_0 sq3b n1_1 sig4a sig4b exp0 mean3 exp1 sq4a sq4b hg3b hg4a n2_0 n2_1 hg4b n3_0 n3_1 mean4 exp2 exp3 n4_0 n4_1 n5_0 exp4 n5_1 n6_0 exp5 n6_1 n7_0 n7_1 exp6 exp7 f7_1",
+    "T": "pm0 pm1 tx0a tx0b tx1a pm2 tx1b z0a pm3 z1a td0a td0b td1a td1b td2a v0a v1a td2b tx2a tx2b tx2c td3a ms0 tx3a tx3b tx3c spread0 tx4a td3b tx4b ms1 s0_0 s0_1 z2a z2b s0_2 v2a v2b s0_3 tx4c spread1 z3a v3a z3b s1_0 v3b s1_1 ms2 s1_2 s1_3 z4a z4b spread2 v4a v4b ms3 s2_0 s2_1 s2_2 s2_3 s3_0 s3_1 s3_2 spread3 s3_3 ms4 s4_0 s4_1 s4_2 s4_3 s5_0 s5_1 spread4 s5_2 s5_3 s6_0 s6_1 s6_2 s6_3 s7_0 s7_1 s7_2 s7_3",
+    "G": "add0 hg0a pow0 add1 pow1 hg1a add2 pow2 add3 pow3 f0_0 add4 f1_0 pow4 f2_0 f3_0 f4_0 f5_0 f6_0 f7_2",
 }
 
 F32 = mybir.dt.float32
@@ -81,6 +81,7 @@ def tile_gated_query_retrieval_f3_kernel(tc, x, wv, bv, wg, bg, gain, docs, log_
         neg_inv_tau = keep.tile([P, TILES], F32, name="neg_inv_tau")
         prior_sb = keep.tile([P, N], BF16, name="prior_sb")
         warm = keep.tile([P, 1], F32, name="warm")
+        warm_pow = keep.tile([P, 2], F32, name="warm_pow")
         mean_sq = keep.tile([P, TILES], F32, name="mean_sq")
         rstd = keep.tile([P, TILES], F32, name="rstd")
         low = keep.tile([P, TILES], F32, name="low")
@@ -374,10 +375,6 @@ def tile_gated_query_retrieval_f3_kernel(tc, x, wv, bv, wg, bg, gain, docs, log_
             nc.scalar.dma_start(out=bv_sb[:], in_=bv.rearrange("(p t) -> p t", t=PACK))
             nc.scalar.dma_start(out=gain_sb[:], in_=gain.rearrange("(p t) -> p t", t=PACK))
             nc.scalar.dma_start(out=prior_row[0:1, :], in_=prior.unsqueeze(0))
-            load_d(0)
-            load_d(1)
-            load_d(2)
-            load_d(3)
             load_w("z", 0)
             load_w("z", 1)
             load_w("z", 2)
@@ -386,12 +383,17 @@ def tile_gated_query_retrieval_f3_kernel(tc, x, wv, bv, wg, bg, gain, docs, log_
             load_w("v", 0)
             load_w("v", 1)
             load_w("v", 2)
+            load_d(0)
+            load_d(1)
+            load_d(2)
+            load_d(3)
             load_x(2)
             load_x(3)
             load_x(4)
             load_x(5)
             load_x(6)
             load_x(7)
+            nc.gpsimd.tensor_tensor(out=warm_pow[:], in0=inv_f[:], in1=minus_half[:], op=ALU.pow)
             nc.scalar.activation(out=inv_tau[:], in_=lt_sb[:], func=ACT.Exp, scale=-1.0)
             nc.scalar.activation(out=warm[:], in_=inv_tau[:, 0:1], func=ACT.Sigmoid)
             nc.gpsimd.tensor_scalar(out=neg_inv_tau[:], in0=inv_tau[:], scalar1=-1.0, scalar2=0.0, op0=ALU.mult, op1=ALU.add)

from contextlib import ExitStack

import concourse.mybir as mybir
from concourse.masks import make_identity

M, K, F, N = 1024, 1536, 512, 2048
FLOPS = 2 * M * K * 2 * F + 2 * M * F * N
P = 128
PACK = 4
KG = K // 512
TILES = M // P
CHUNK = 512
CHUNKS = N // CHUNK
GROUP_SIZES = (1, 1, 2, 2, 2)
NARROW = (2, 2, 2, 2, 2, 2, 2, 2)
LIFT = (((0, 2048, "G"),), ((0, 2048, "G"),), ((0, 2048, "G"),), ((0, 2048, "G"),), ((0, 2048, "G"),), ((0, 2048, "G"),), ((0, 2048, "G"),), ((0, 1024, "V"), (1024, 1536, "S"), (1536, 2048, "G")))
WENG = "VVVSVS"
XENG = "SSSSS"
DENG = "SSSSSSSS"
EENG = "VVVVV"
HENG = "GGSSS"
NENG = "S"
PREADD = 1
ORDER = {
    "V": "Iz0 Iz1 Qz0 Qz1 Iz2 xq0a xq0b Qz2 xq1a xq1b Iv1 pc0 Qv0 Qv1 pc2 Qv2 dq0 h0a dq1 h1a e0 xq2a qe0 xq2b xq2c xq3a dq2 l0_0 xq3b xq3c xq4a l0_1 dq3 l0_2 h2a h2b l0_3 e1 xq4b qe1 lw0 h3a l1_0 ln0 xq4c h3b l1_1 l1_2 l1_3 lw1 e2 h4a qe2 ln1 h4b l2_0 l2_1 inv0 l2_2 l2_3 l3_0 l3_1 l3_2 lw2 e3 inv1 qe3 l3_3 ln2 lw3 l4_0 ln3 l4_1 inv2 l4_2 l4_3 e4 inv3 lw4 l5_0 ln4 l5_1 l5_2 l5_3 qe4 lw5 inv4 l6_0 ln5 l6_1 l6_2 l6_3 l7_0 lw6 l7_1 ln6 l7_2 l7_3 inv5 lw7 ln7 inv6 inv7 f7_0",
    "S": "pc1 cx0a cx0b cx1a cx1b Iv0 Iv2 cd0a cd0b cd1a sig0a cd1b sig1a sq0a sq1a cx2a cx2b cd2a mean0 cd2b cd3a pc3 cx2c cx3a cd3b cx3b cx3c cx4a mean1 n0_0 sig2a n0_1 cx4b sig2b sq2a hg2a sq2b sig3a hg2b cx4c sig3b sq3a hg3a mean2 n1_0 sq3b n1_1 sig4a sig4b exp0 mean3 exp1 sq4a sq4b hg3b hg4a n2_0 n2_1 hg4b n3_0 n3_1 mean4 exp2 exp3 n4_0 n4_1 n5_0 exp4 n5_1 n6_0 exp5 n6_1 n7_0 n7_1 exp6 exp7 f7_1",
    "T": "pm0 pm1 tx0a tx0b tx1a pm2 tx1b z0a pm3 z1a td0a td0b td1a td1b td2a v0a v1a td2b tx2a tx2b tx2c td3a ms0 tx3a tx3b tx3c spread0 tx4a td3b tx4b ms1 s0_0 s0_1 z2a z2b s0_2 v2a v2b s0_3 tx4c spread1 z3a v3a z3b s1_0 v3b s1_1 ms2 s1_2 s1_3 z4a z4b spread2 v4a v4b ms3 s2_0 s2_1 s2_2 s2_3 s3_0 s3_1 s3_2 spread3 s3_3 ms4 s4_0 s4_1 s4_2 s4_3 s5_0 s5_1 spread4 s5_2 s5_3 s6_0 s6_1 s6_2 s6_3 s7_0 s7_1 s7_2 s7_3",
    "G": "add0 hg0a pow0 add1 pow1 hg1a add2 pow2 add3 pow3 f0_0 add4 f1_0 pow4 f2_0 f3_0 f4_0 f5_0 f6_0 f7_2",
}

F32 = mybir.dt.float32
BF16 = mybir.dt.bfloat16
U32 = mybir.dt.uint32
U8 = mybir.dt.uint8
E4M3X4 = mybir.dt.float8_e4m3fn_x4
E5M2X4 = mybir.dt.float8_e5m2_x4
ALU = mybir.AluOpType
ACT = mybir.ActivationFunctionType


def tile_gated_query_retrieval_f3_kernel(tc, x, wv, bv, wg, bg, gain, docs, log_tau, prior, out):
    nc = tc.nc
    x_rows = x.rearrange("(p t) k -> t p k", t=TILES)
    out_rows = out.rearrange("(p t) n -> t p n", t=TILES)
    w_rows = {"z": wg.rearrange("(g p j) f -> g p j f", p=P, j=PACK), "v": wv.rearrange("(g p j) f -> g p j f", p=P, j=PACK)}
    doc_rows = docs.rearrange("(c r p) f -> c p r f", c=CHUNKS, p=P)
    groups = []
    for n in GROUP_SIZES:
        groups.append((sum(GROUP_SIZES[:len(groups)]), n))
    where = {}
    for g, (first, n) in enumerate(groups):
        for b in range(n):
            where[first + b] = (g, b)

    with ExitStack() as ctx:
        keep = ctx.enter_context(tc.tile_pool(name="keep", bufs=1))
        work = ctx.enter_context(tc.tile_pool(name="work", bufs=2))
        raw = ctx.enter_context(tc.tile_pool(name="raw", bufs=8))
        soft = ctx.enter_context(tc.tile_pool(name="soft", bufs=2))
        lots = ctx.enter_context(tc.tile_pool(name="lots", bufs=4))
        banks = ctx.enter_context(tc.psum_pool(name="banks", bufs=7))
        rms = ctx.enter_context(tc.psum_pool(name="rms", bufs=1))

        prior_row = raw.tile([P, N], BF16, name="prior_row", tag="raw", align_bytes=64)
        nc.vector.memset(prior_row[:], 0.0)
        ones = keep.tile([P, P], BF16, name="ones")
        nc.vector.memset(ones[:], 1.0)
        ident = keep.tile([P, P], F32, name="ident")
        make_identity(nc, ident[:])
        inv_f = keep.tile([P, 2], F32, name="inv_f")
        nc.gpsimd.memset(inv_f[:], 1.0 / F)
        minus_half = keep.tile([P, 2], F32, name="minus_half")
        nc.gpsimd.memset(minus_half[:], -0.5)

        bv_sb = keep.tile([P, PACK], BF16, name="bv_sb")
        bg_sb = keep.tile([P, PACK], BF16, name="bg_sb")
        gain_sb = keep.tile([P, PACK], BF16, name="gain_sb")
        gain32 = keep.tile([P, PACK], F32, name="gain32")
        lt_sb = keep.tile([P, TILES], BF16, name="lt_sb")
        inv_tau = keep.tile([P, TILES], F32, name="inv_tau")
        neg_inv_tau = keep.tile([P, TILES], F32, name="neg_inv_tau")
        prior_sb = keep.tile([P, N], BF16, name="prior_sb")
        warm = keep.tile([P, 1], F32, name="warm")
        warm_pow = keep.tile([P, 2], F32, name="warm_pow")
        mean_sq = keep.tile([P, TILES], F32, name="mean_sq")
        rstd = keep.tile([P, TILES], F32, name="rstd")
        low = keep.tile([P, TILES], F32, name="low")
        part_low = keep.tile([P, TILES], F32, name="part_low")
        total = keep.tile([P, TILES], F32, name="total")
        share = keep.tile([P, TILES], F32, name="share")
        scaled = keep.tile([P, TILES], F32, name="scaled")

        w_raw, d_raw, w_grp, w_codes, w_scales = {}, {}, {}, {}, {}
        for which in ("z", "v"):
            for g in range(KG):
                tagname = "%s%d" % (which, g)
                w_codes[which, g] = keep.tile([P, F], U32, name="w_codes_" + tagname, align_bytes=64)
                w_scales[which, g] = keep.tile([P, F], U8, name="w_scales_" + tagname, align_bytes=64)
        x_raw = {}
        x_codes = [keep.tile([P, KG, n * P], U32, name="x_codes%d" % g, align_bytes=64) for g, (first, n) in enumerate(groups)]
        x_scales = [keep.tile([P, KG, n * P], U8, name="x_scales%d" % g, align_bytes=64) for g, (first, n) in enumerate(groups)]
        d_codes = [keep.tile([P, CHUNK], U32, name="d_codes%d" % c, align_bytes=64) for c in range(CHUNKS)]
        d_scales = [keep.tile([P, CHUNK], U8, name="d_scales%d" % c, align_bytes=64) for c in range(CHUNKS)]
        e_codes = [keep.tile([P, n * P], U32, name="e_codes%d" % g, align_bytes=64) for g, (first, n) in enumerate(groups)]
        e_scales = [keep.tile([P, n * P], U8, name="e_scales%d" % g, align_bytes=64) for g, (first, n) in enumerate(groups)]
        bank_of, grp_of, sig, h, hg, sq, sums, bc, bcs, e_bf, d_grp, neg, nb, pb = {}, {}, {}, {}, {}, {}, {}, {}, {}, {}, {}, {}, {}, {}
        copy_on = {"V": nc.vector.tensor_copy, "S": nc.scalar.copy}

        def load_w(which, g):
            w_raw[which, g] = raw.tile([P, PACK, F], BF16, name="raw", align_bytes=64)
            nc.sync.dma_start(out=w_raw[which, g][:], in_=w_rows[which][g])

        def load_x(i):
            x_raw[i] = raw.tile([P, K], BF16, name="x_raw", bufs=6, align_bytes=64)
            nc.sync.dma_start(out=x_raw[i][:], in_=x_rows[i])

        def load_d(c):
            d_raw[c] = raw.tile([P, 4, F], BF16, name="raw", align_bytes=64)
            nc.sync.dma_start(out=d_raw[c][:], in_=doc_rows[c])

        def spread_prior(c):
            pb[c] = banks.tile([P, CHUNK], F32, name="bank_p", tag="bank")
            nc.tensor.matmul(out=pb[c][:], lhsT=ones[:], rhs=prior_row[:, c * CHUNK:(c + 1) * CHUNK], start=True, stop=True)

        def copy_prior(c):
            copy_on["VS"[c % 2]](out=prior_sb[:, c * CHUNK:(c + 1) * CHUNK], in_=pb[c][:])

        def interleave(which, g, engine):
            w_grp[which, g] = soft.tile([P, F * PACK], BF16, name="w_grp", tag="w_grp" + engine, bufs=3 if engine == "V" else 2, align_bytes=64)
            copy_on[engine](out=w_grp[which, g][:].rearrange("p (t m j) -> p t m j", t=PACK, j=PACK),
                 in_=w_raw[which, g][:].rearrange("p j (m t) -> p t m j", t=PACK))

        def quant_w(which, g):
            nc.vector.quantize_mx(out=w_codes[which, g][:].bitcast(E4M3X4), scales=w_scales[which, g][:], in_=w_grp[which, g][:])

        def slots_of(g, k):
            n = groups[g][1]
            if n == 2:
                return [(k, 0), (k, 1)]
            return [(0, 0), (1, 0)] if k == 0 else [(2, 0)]

        def turn_x(g, k):
            slots = slots_of(g, k)
            bank = banks.tile([P, len(slots), 2, P], F32, name="bank_x", tag="bank")
            for s, (kg, b) in enumerate(slots):
                words = x_raw[groups[g][0] + b][:].bitcast(F32)
                for u in range(2):
                    nc.tensor.transpose(bank[:, s, u, :], words[:, 256 * kg + u:256 * (kg + 1):2], ident[:])
            bank_of["x", g, k] = bank

        def copy_x(g, k):
            n = len(slots_of(g, k))
            grp_of[g, k] = work.tile([P, n * P * PACK], BF16, name="x_grp", bufs=4, align_bytes=64)
            copy_on[XENG[g]](out=grp_of[g, k][:].bitcast(F32).rearrange("p (c r u) -> p c r u", c=n, u=2), in_=bank_of["x", g, k][:].rearrange("p c u r -> p c r u"))

        def quant_x(g, k):
            if groups[g][1] == 2:
                codes, scales = x_codes[g][:, k, :], x_scales[g][:, k, :]
            else:
                kg = slice(0, 2) if k == 0 else slice(2, 3)
                codes, scales = x_codes[g][:, kg, :].rearrange("p g m -> p (g m)"), x_scales[g][:, kg, :].rearrange("p g m -> p (g m)")
            nc.vector.quantize_mx(out=codes.bitcast(E4M3X4), scales=scales, in_=grp_of[g, k][:])

        def project(which, g, part):
            n = groups[g][1]
            m = PACK // n
            bank = banks.tile([P, m, n * P], F32, name="bank_" + which, tag="bank")
            for s in range(m):
                t = part * m + s
                cols = slice(t * P, (t + 1) * P)
                for k in range(KG):
                    nc.tensor.matmul_mx(
                        out=bank[:, s, :],
                        lhsT=w_codes[which, k][:, cols].bitcast(E4M3X4), lhsT_scale=w_scales[which, k][:, cols],
                        rhs=x_codes[g][:, k, :].bitcast(E4M3X4), rhs_scale=x_scales[g][:, k, :],
                        start=(k == 0), stop=(k == KG - 1))
            bank_of[which, g, part] = bank

        def rows_of(store, g, name, bufs):
            if g not in store:
                store[g] = work.tile([P, PACK, groups[g][1] * P], F32, name=name, tag="%s%d" % (name, groups[g][1]), bufs=bufs[groups[g][1] - 1])
            return store[g]

        def each_t(g, part):
            m = PACK // groups[g][1]
            return [(part * m + s, s) for s in range(m)]

        def sigmoid(g, part):
            to = rows_of(sig, g, "sig", (2, 3))
            for t, s in each_t(g, part):
                nc.scalar.activation(out=to[:, t, :], in_=bank_of["z", g, part][:, s, :], func=ACT.Sigmoid, bias=bg_sb[:, t:t + 1])

        def gate(g, part):
            to = rows_of(h, g, "h", (2, 2))
            for t, s in each_t(g, part):
                nc.vector.scalar_tensor_tensor(out=to[:, t, :], in0=bank_of["v", g, part][:, s, :], scalar=bv_sb[:, t:t + 1], in1=sig[g][:, t, :], op0=ALU.add, op1=ALU.mult)

        def gained(g, part):
            to = rows_of(hg, g, "hg", (2, 2))
            for t, s in each_t(g, part):
                if HENG[g] == "G":
                    nc.gpsimd.tensor_scalar(out=to[:, t, :], in0=h[g][:, t, :], scalar1=gain_sb[:, t:t + 1], scalar2=0.0, op0=ALU.mult, op1=ALU.add)
                else:
                    nc.scalar.activation(out=to[:, t, :], in_=h[g][:, t, :], func=ACT.Copy, scale=gain32[:, t:t + 1])

        def square(g, part):
            to = rows_of(sq, g, "sq", (2, 2))
            m = PACK // groups[g][1]
            nc.scalar.activation(out=to[:, part * m:(part + 1) * m, :], in_=h[g][:, part * m:(part + 1) * m, :], func=ACT.Square)

        def add_up(g):
            n = groups[g][1]
            half = work.tile([P, 2, n * P], F32, name="half", tag="half%d" % n, bufs=1)
            nc.gpsimd.tensor_tensor(out=half[:], in0=sq[g][:, 0:2, :], in1=sq[g][:, 2:4, :], op=ALU.add)
            sums[g] = work.tile([P, n * P], F32, name="sums", tag="sums%d" % n)
            nc.gpsimd.tensor_tensor(out=sums[g][:], in0=half[:, 0, :], in1=half[:, 1, :], op=ALU.add)

        def mean_square(g):
            n = groups[g][1]
            bc[g] = rms.tile([P, 2 * P + 2], F32, name="bc")
            for b in range(n):
                parts = [sums[g][:, b * P:(b + 1) * P]] if PREADD else [sq[g][:, t, b * P:(b + 1) * P] for t in range(PACK)]
                for t in range(len(parts)):
                    nc.tensor.matmul(out=bc[g][:, 2 * P + b:2 * P + b + 1], lhsT=parts[t], rhs=inv_f[:, 0:1], start=(t == 0), stop=(t == len(parts) - 1))

        def mean_copy(g):
            first, n = groups[g]
            nc.scalar.copy(out=mean_sq[:, first:first + n], in_=bc[g][:, 2 * P:2 * P + n])

        def raise_power(g):
            first, n = groups[g]
            nc.gpsimd.tensor_tensor(out=rstd[:, first:first + n], in0=mean_sq[:, first:first + n], in1=minus_half[:, 0:n], op=ALU.pow)

        def spread(g):
            first, n = groups[g]
            for b in range(n):
                nc.tensor.matmul(out=bc[g][:, b * P:(b + 1) * P], lhsT=rstd[:, first + b:first + b + 1].to_broadcast([P, P]), rhs=ident[:], start=True, stop=True)

        def carry(g):
            w = groups[g][1] * P
            bcs[g] = work.tile([P, w], F32, name="bcs", tag="bcs%d" % groups[g][1])
            nc.scalar.copy(out=bcs[g][:], in_=bc[g][:, 0:w])

        def embed(g):
            w = groups[g][1] * P
            e_bf[g] = work.tile([P, w, PACK], BF16, name="e_bf", tag="e_bf%d" % groups[g][1], align_bytes=64)
            engine, factor = (nc.vector, bc[g]) if EENG[g] == "V" else (nc.gpsimd, bcs[g])
            engine.tensor_tensor(out=e_bf[g][:], in0=hg[g][:].rearrange("p t n -> p n t"), in1=factor[:, 0:w].unsqueeze(2).to_broadcast([P, w, PACK]), op=ALU.mult)

        def quant_e(g):
            nc.vector.quantize_mx(out=e_codes[g][:].bitcast(E5M2X4), scales=e_scales[g][:], in_=e_bf[g][:].rearrange("p n t -> p (n t)"))

        def turn_d(c, half):
            bank = banks.tile([P, 2, 2, P], F32, name="bank_d", tag="bank")
            for b in range(2):
                words = d_raw[c][:, 2 * half + b, :].bitcast(F32)
                for u in range(2):
                    nc.tensor.transpose(bank[:, b, u, :], words[:, u:256:2], ident[:])
            bank_of["d", c, half] = bank

        def copy_d(c, half):
            if c not in d_grp:
                d_grp[c] = work.tile([P, CHUNK * PACK], BF16, name="d_grp", align_bytes=64)
            copy_on[DENG[2 * c + half]](out=d_grp[c][:, half * 1024:(half + 1) * 1024].bitcast(F32).rearrange("p (b r u) -> p b r u", b=2, u=2), in_=bank_of["d", c, half][:].rearrange("p b u r -> p b r u"))

        def quant_d(c):
            nc.vector.quantize_mx(out=d_codes[c][:].bitcast(E4M3X4), scales=d_scales[c][:], in_=d_grp[c][:])

        def score(i, c):
            g, b = where[i]
            cols = slice(b * P, (b + 1) * P)
            bank_of["s", i, c] = banks.tile([P, CHUNK], F32, name="bank_s", tag="bank")
            nc.tensor.matmul_mx(out=bank_of["s", i, c][:], lhsT=e_codes[g][:, cols].bitcast(E5M2X4), lhsT_scale=e_scales[g][:, cols],
                                rhs=d_codes[c][:].bitcast(E4M3X4), rhs_scale=d_scales[c][:], start=True, stop=True)

        def logit(i, c):
            if i not in neg:
                neg[i] = lots.tile([P, N], F32, name="neg")
            cols = slice(c * CHUNK, (c + 1) * CHUNK)
            nc.vector.scalar_tensor_tensor(out=neg[i][:, cols], in0=bank_of["s", i, c][:], scalar=neg_inv_tau[:, i:i + 1], in1=prior_sb[:, cols], op0=ALU.mult, op1=ALU.subtract)

        def narrow(i, c):
            if i not in nb:
                nb[i] = soft.tile([P, NARROW[i] * CHUNK], BF16, name="nb", tag="nb%d" % NARROW[i])
            cols = slice(c * CHUNK, (c + 1) * CHUNK)
            if NENG == "S":
                nc.scalar.copy(out=nb[i][:, cols], in_=neg[i][:, cols])
            else:
                nc.gpsimd.tensor_scalar(out=nb[i][:, cols], in0=neg[i][:, cols], scalar1=1.0, scalar2=0.0, op0=ALU.mult, op1=ALU.add)

        def low_wide(i):
            to = part_low if NARROW[i] else low
            nc.vector.tensor_reduce(out=to[:, i:i + 1], in_=neg[i][:, NARROW[i] * CHUNK:N], axis=mybir.AxisListType.X, op=ALU.min)

        def low_narrow(i):
            start = part_low[:, i:i + 1] if NARROW[i] < CHUNKS else None
            nc.vector.tensor_scalar(out=nb[i][:], in0=nb[i][:], scalar1=1.0, scalar2=start, op0=ALU.mult, op1=ALU.min, accum_out=low[:, i:i + 1])

        def exponent(i):
            nc.scalar.activation(out=neg[i][:], in_=neg[i][:], func=ACT.Exp, scale=-1.0, bias=low[:, i:i + 1], accum_out=total[:, i:i + 1])

        def invert(i):
            nc.vector.reciprocal(out=share[:, i:i + 1], in_=total[:, i:i + 1])
            if any(cut[2] == "S" for cut in LIFT[i]):
                nc.vector.tensor_scalar(out=scaled[:, i:i + 1], in0=share[:, i:i + 1], scalar1=float(N), scalar2=0.0, op0=ALU.mult, op1=ALU.add)

        def lift(i, k):
            lo, hi, engine = LIFT[i][k]
            a = neg[i][:, lo:hi]
            if engine == "S":
                nc.scalar.activation(out=a, in_=a, func=ACT.Copy, scale=scaled[:, i:i + 1])
            else:
                (nc.vector if engine == "V" else nc.gpsimd).tensor_scalar(out=a, in0=a, scalar1=share[:, i:i + 1], scalar2=float(N), op0=ALU.mult, op1=ALU.mult)
            nc.sync.dma_start(out=out_rows[i][:, lo:hi], in_=a)

        needs, emit = {}, {}

        def piece(name, deps, f, *args):
            emit[name] = (f, args)
            needs[name] = deps

        for c in range(CHUNKS):
            piece("pm%d" % c, [], spread_prior, c)
            piece("pc%d" % c, ["pm%d" % c], copy_prior, c)
        for k in range(6):
            which, g = "zv"[k // 3], k % 3
            w = "%s%d" % (which, g)
            piece("I" + w, [], interleave, which, g, WENG[k])
            piece("Q" + w, ["I" + w], quant_w, which, g)
        for g, (first, n) in enumerate(groups):
            name = str(g)
            turns = range(3) if n == 2 else range(2)
            for k in turns:
                piece("tx" + name + "abc"[k], [], turn_x, g, k)
                piece("cx" + name + "abc"[k], ["tx" + name + "abc"[k]], copy_x, g, k)
                piece("xq" + name + "abc"[k], ["cx" + name + "abc"[k]], quant_x, g, k)
            ready = ["xq" + name + "abc"[k] for k in turns]
            parts = ["ab"[b] for b in range(n)]
            for b, a in enumerate(parts):
                for which in "zv":
                    piece(which + name + a, ready + ["Q%s%d" % (which, k) for k in range(KG)], project, which, g, b)
                piece("sig" + name + a, ["z" + name + a], sigmoid, g, b)
                piece("h" + name + a, ["v" + name + a, "sig" + name + a], gate, g, b)
                piece("hg" + name + a, ["h" + name + a], gained, g, b)
                piece("sq" + name + a, ["h" + name + a], square, g, b)
            piece("add" + name, ["sq" + name + a for a in parts], add_up, g)
            piece("ms" + name, ["add" + name] if PREADD else ["sq" + name + a for a in parts], mean_square, g)
            piece("mean" + name, ["ms" + name], mean_copy, g)
            piece("pow" + name, ["mean" + name], raise_power, g)
            piece("spread" + name, ["pow" + name], spread, g)
            piece("carry" + name, ["spread" + name], carry, g)
            piece("e" + name, [("spread" if EENG[g] == "V" else "carry") + name] + ["hg" + name + a for a in parts], embed, g)
            piece("qe" + name, ["e" + name], quant_e, g)
            for i in range(first, first + n):
                for c in range(CHUNKS):
                    piece("s%d_%d" % (i, c), ["qe" + name, "dq%d" % c], score, i, c)
                    piece("l%d_%d" % (i, c), ["s%d_%d" % (i, c), "pc%d" % c], logit, i, c)
                    piece("n%d_%d" % (i, c), ["l%d_%d" % (i, c)], narrow, i, c)
                piece("lw%d" % i, ["l%d_%d" % (i, c) for c in range(NARROW[i], CHUNKS)], low_wide, i)
                piece("ln%d" % i, ["n%d_%d" % (i, c) for c in range(NARROW[i])] + (["lw%d" % i] if NARROW[i] < CHUNKS else []), low_narrow, i)
                piece("exp%d" % i, [("ln%d" if NARROW[i] else "lw%d") % i], exponent, i)
                piece("inv%d" % i, ["exp%d" % i], invert, i)
                for k in range(len(LIFT[i])):
                    piece("f%d_%d" % (i, k), ["inv%d" % i], lift, i, k)
        for c in range(CHUNKS):
            for half in range(2):
                hn = "%d%s" % (c, "ab"[half])
                piece("td" + hn, [], turn_d, c, half)
                piece("cd" + hn, ["td" + hn], copy_d, c, half)
            piece("dq%d" % c, ["cd%da" % c, "cd%db" % c], quant_d, c)

        with tc.manual_schedule():
            nc.scalar.dma_start(out=lt_sb[:], in_=log_tau.rearrange("(p t) -> p t", t=TILES))
            nc.scalar.dma_start(out=bg_sb[:], in_=bg.rearrange("(p t) -> p t", t=PACK))
            nc.scalar.dma_start(out=bv_sb[:], in_=bv.rearrange("(p t) -> p t", t=PACK))
            nc.scalar.dma_start(out=gain_sb[:], in_=gain.rearrange("(p t) -> p t", t=PACK))
            nc.scalar.dma_start(out=prior_row[0:1, :], in_=prior.unsqueeze(0))
            load_w("z", 0)
            load_w("z", 1)
            load_w("z", 2)
            load_x(0)
            load_x(1)
            load_w("v", 0)
            load_w("v", 1)
            load_w("v", 2)
            load_d(0)
            load_d(1)
            load_d(2)
            load_d(3)
            load_x(2)
            load_x(3)
            load_x(4)
            load_x(5)
            load_x(6)
            load_x(7)
            nc.gpsimd.tensor_tensor(out=warm_pow[:], in0=inv_f[:], in1=minus_half[:], op=ALU.pow)
            nc.scalar.activation(out=inv_tau[:], in_=lt_sb[:], func=ACT.Exp, scale=-1.0)
            nc.scalar.activation(out=warm[:], in_=inv_tau[:, 0:1], func=ACT.Sigmoid)
            nc.gpsimd.tensor_scalar(out=neg_inv_tau[:], in0=inv_tau[:], scalar1=-1.0, scalar2=0.0, op0=ALU.mult, op1=ALU.add)
            nc.gpsimd.tensor_copy(out=gain32[:], in_=gain_sb[:])
            queues = {e: names.split() for e, names in ORDER.items()}
            done = set()
            left = sum(len(q) for q in queues.values())
            while left:
                before = left
                for e in queues:
                    while queues[e] and all(d in done for d in needs[queues[e][0]]):
                        name = queues[e].pop(0)
                        f, args = emit[name]
                        f(*args)
                        done.add(name)
                        left -= 1
                assert left < before
